import numpy as np
import ml_dtypes


def mxq(x, axis, fmt="e4m3"):
    dtype, down = {"e4m3": (ml_dtypes.float8_e4m3fn, 7), "e5m2": (ml_dtypes.float8_e5m2, 14)}[fmt]
    v = np.moveaxis(np.asarray(x, np.float32).astype(ml_dtypes.bfloat16).astype(np.float64), axis, -1)
    blocks = v.reshape(v.shape[:-1] + (-1, 32))
    amax = np.abs(blocks).max(-1, keepdims=True)
    byte = np.maximum(np.where(amax > 0, np.frexp(amax)[1] - 1 + 127, 0) - down, 1)
    scale = np.exp2(byte - 127.0)
    codes = (blocks / scale).astype(np.float32).astype(dtype).astype(np.float64)
    return np.moveaxis((codes * scale).reshape(v.shape), -1, axis)


WIDE = False


def mx_kscale(k):
    if not WIDE:
        return np.ones(k)
    levels = np.array([30, -30])
    if k % 512:
        return np.exp2(np.random.permutation(np.resize(levels, k // 32))).repeat(32)
    a = np.empty((k // 512, 16))
    for p in range(k // 512):
        a[p, :8] = np.random.permutation(np.resize(levels, 8))
        for g in range(8):
            far = levels[np.abs(levels - a[p, g]) >= 10]
            a[p, g + 8] = far[np.random.randint(len(far))]
    return np.exp2(a.ravel()).repeat(32)


def f64(x):
    return np.asarray(x).astype(np.float64)


def striped(idx):
    return np.tile(np.asarray(idx).reshape(-1, 16).T, (8, 1)).astype(np.uint16)


def unstriped(offs):
    return offs[:16].T.reshape(-1).astype(np.int64)


E2M1 = np.array([0.0, 0.5, 1.0, 1.5, 2.0, 3.0, 4.0, 6.0, -0.0, -0.5, -1.0, -1.5, -2.0, -3.0, -4.0, -6.0])


def pack_weight(w, fmt):
    k, n = w.shape
    w = f64(np.asarray(w, np.float32).astype(ml_dtypes.bfloat16)).reshape(k // 32, 32, n)
    amax = np.abs(w).max(1)
    if fmt == "e4m3":
        byte = np.frexp(amax)[1] - 1 + 127 - 7
    else:
        mant, ex = np.frexp(amax / 6.0)
        byte = np.where(mant > 0.5, ex, ex - 1) + 127
    byte = np.clip(np.where(amax > 0, byte, 1), 1, 254)
    scaled = (w * np.exp2(127.0 - byte)[:, None, :]).reshape(k, n).astype(np.float32)
    by_word = np.ascontiguousarray(scaled.reshape(k // 512, 128, 4, n).transpose(0, 1, 3, 2))
    if fmt == "e4m3":
        words = by_word.astype(ml_dtypes.float8_e4m3fn).view(np.uint8)
    else:
        c = by_word.astype(ml_dtypes.float4_e2m1fn).view(np.uint8) & 0xF
        words = (c[..., 0::2] | (c[..., 1::2] << 4)).reshape(k // 512, 128, 2 * n)
    return np.ascontiguousarray(words), np.ascontiguousarray(byte.astype(np.uint8).reshape(k // 512, 16, n))


def unpack_weight(words, scales, fmt):
    g, _, n = scales.shape
    words = np.ascontiguousarray(words).reshape(g, 128, n, -1)
    if fmt == "e4m3":
        vals = words.view(ml_dtypes.float8_e4m3fn).astype(np.float64)
    else:
        nib = np.empty((g, 128, n, 4), np.uint8)
        nib[..., 0::2] = words & 0xF
        nib[..., 1::2] = words >> 4
        vals = E2M1[nib]
    vals = vals * np.repeat(np.exp2(scales.astype(np.float64) - 127.0), 8, axis=1)[..., None]
    return vals.transpose(0, 1, 3, 2).reshape(g * 512, n)


K, J, N, R, T, V, C = 512, 512, 256, 256, 1024, 1024, 64


def setup_inputs():
    n = np.random.standard_normal
    idx = np.random.permutation(T)[:J]
    idx2 = np.random.permutation(V)[:J]
    fj = mx_kscale(J)
    fk = mx_kscale(K)
    drp = pack_weight(n((K, R)) * 1 / np.sqrt(K) / fk[:, None], "e2m1")
    return {
        "xf": (n((K, T)) * np.random.uniform(0.4, 1.6, (1, T))).astype(np.float32),
        "ca": (np.random.uniform(0.5, 1.5, (J, 1)) * fj[:, None]).astype(np.float32),
        "gt": (n((N, V)) * np.exp(0.5 * n((1, V)))).astype(np.float32),
        "rb": (np.random.uniform(0.5, 1.5, (1, J)) / fj).astype(np.float32),
        "fkr": (np.random.uniform(0.5, 1.5, (1, K)) * fk).astype(np.float32),
        "dr_words": drp[0],
        "dr_scales": drp[1],
        "old": (1.0 * n((R, N))).astype(np.float32),
        "offs": striped(idx),
        "offs2": striped(idx2),
    }


def reference(xf, ca, gt, rb, fkr, dr_words, dr_scales, old, offs, offs2):
    idx = unstriped(offs)
    idx2 = unstriped(offs2)
    dru = unpack_weight(dr_words, dr_scales, "e2m1")
    xj = f64(xf)[:, idx].T
    uj = xj / (np.mean(np.abs(xj), axis=1, keepdims=True) + 0.1) * f64(ca) * f64(fkr)
    gg = f64(gt)[:, idx2]
    c1 = gg.reshape(N, C, J // C).mean(axis=2)
    c2 = np.repeat(c1, J // C, axis=1)
    gs = (gg - c2) * f64(rb)
    gj = gs.T
    ujq = mxq(uj, 0, "e4m3")
    gjq = mxq(gj, 0, "e5m2")
    w = ujq.T @ gjq
    wq = mxq(w, 0, "e5m2")
    v2 = dru.T @ wq
    y = 0.05 * v2 + 0.5 * f64(old)
    return y

@@ -1,0 +1,156 @@
+from contextlib import ExitStack
+
+import concourse.mybir as mybir
+from concourse.masks import make_identity
+
+K, J, N, R, T = 512, 512, 256, 256, 1024
+FLOPS = 2 * J * K * N + 2 * K * R * N
+
+F32 = mybir.dt.float32
+BF16 = mybir.dt.bfloat16
+I32 = mybir.dt.int32
+U32 = mybir.dt.uint32
+U16 = mybir.dt.uint16
+U8 = mybir.dt.uint8
+E4M3 = mybir.dt.float8_e4m3fn_x4
+E5M2 = mybir.dt.float8_e5m2_x4
+E2M1 = mybir.dt.float4_e2m1fn_x4
+ALU = mybir.AluOpType
+ACT = mybir.ActivationFunctionType
+AX = mybir.AxisListType
+
+P = 128
+PACK = 4
+SET = 8
+VCOLS = 20
+
+
+def tile_list_directions_sized_centred_mixed_kernel(tc, xf, ca, gt, rb, fkr, dr_words, dr_scales, old, offs, offs2, out):
+    nc = tc.nc
+    with ExitStack() as ctx:
+        sb = ctx.enter_context(tc.tile_pool(name="sb", bufs=1))
+        ps = ctx.enter_context(tc.psum_pool(name="ps", bufs=1))
+
+        xlist = sb.tile([P, J // 16], U16, name="xlist")
+        glist = sb.tile([P, J // 16], U16, name="glist")
+        xwin = [sb.tile([P, T], F32, name=f"xwin{t}") for t in range(PACK)]
+        gwin = [sb.tile([P, T], F32, name=f"gwin{h}") for h in range(2)]
+        fk = sb.tile([P, PACK], F32, name="fk")
+        cj = sb.tile([P, PACK], F32, name="cj")
+        rj = sb.tile([P, PACK], F32, name="rj")
+        oldt = sb.tile([P, 2, N], F32, name="oldt")
+        dwords = sb.tile([P, 2 * R], U8, name="dwords", align_bytes=64)
+        dplane = sb.tile([P, R], U8, name="dplane", align_bytes=64)
+        ident = sb.tile([P, P], F32, name="ident")
+
+        xrows = xf.rearrange("(p t) c -> t p c", t=PACK)
+        nc.sync.dma_start(xlist[:], offs)
+        nc.sync.dma_start(xwin[0][:], xrows[0])
+        nc.scalar.dma_start(fk[:], fkr.rearrange("o (p t) -> p (o t)", t=PACK))
+        for t in range(1, PACK):
+            nc.sync.dma_start(xwin[t][:], xrows[t])
+        nc.sync.dma_start(glist[:], offs2)
+        nc.sync.dma_start(gwin[0][:], gt[0:P, :])
+        nc.sync.dma_start(cj[:], ca.rearrange("(p s) o -> p (s o)", s=PACK))
+        nc.sync.dma_start(gwin[1][:], gt[P:2 * P, :])
+        nc.sync.dma_start(rj[:], rb.rearrange("o (p s) -> p (o s)", s=PACK))
+        nc.sync.dma_start(oldt[:], old.rearrange("(a p) n -> p a n", p=P))
+        nc.sync.dma_start(dwords[:].bitcast(I32), dr_words[0].bitcast(I32))
+        make_identity(nc, ident[:])
+        nc.gpsimd.memset(dplane[:].bitcast(I32), 0)
+        for q in range(4):
+            nc.sync.dma_start(dplane[32 * q:32 * q + 4, :].bitcast(I32), dr_scales[0, 4 * q:4 * q + 4, :].bitcast(I32))
+
+        ubank = [ps.tile([P, PACK, P], F32, name=f"ubank{t}", tag=f"u{t}") for t in range(PACK)]
+        abank = ps.tile([P, PACK, P], F32, name="abank", tag="a")
+        nv = 16 * VCOLS
+        for t in range(PACK):
+            xg = sb.tile([P, J], F32, name=f"xg{t}")
+            nc.vector.tensor_copy(xg[:, :nv], xwin[t][:].indirect(xlist[:, :VCOLS]))
+            nc.scalar.activation(xg[:, nv:], xwin[t][:].indirect(xlist[:, VCOLS:]), ACT.Copy)
+            by_slot = xg[:].rearrange("p (q s) -> p q s", s=PACK)
+            xa = sb.tile([P, PACK, P], F32, name=f"xa{t}")
+            nc.scalar.activation(xa[:].rearrange("p s q -> p q s"), by_slot, ACT.Abs, scale=1.0 / K)
+            xs = sb.tile([P, PACK, P], F32, name=f"xs{t}")
+            nc.vector.tensor_scalar(xs[:].rearrange("p s q -> p q s"), by_slot, fk[:, t:t + 1], None, ALU.mult)
+            for s in range(PACK):
+                nc.tensor.matmul(abank[:, s, :], xa[:, s, :], ident[:], is_transpose=True,
+                                 start=(t == 0 and s == 0), stop=(t == PACK - 1 and s == PACK - 1))
+            for s in range(PACK):
+                nc.tensor.transpose(ubank[t][:, s, :], xs[:, s, :], ident[:])
+
+        gg = []
+        for h in range(2):
+            g = sb.tile([P, J], F32, name=f"gg{h}")
+            nc.scalar.activation(g[:], gwin[h][:].indirect(glist[:]), ACT.Copy)
+            gg.append(g)
+
+        mean = sb.tile([P, PACK], F32, name="mean")
+        nc.vector.tensor_reduce(mean[:], abank[:], AX.X, ALU.add)
+        den = sb.tile([P, PACK], F32, name="den")
+        nc.vector.tensor_scalar(den[:], mean[:], 0.1, None, ALU.add)
+        rec = sb.tile([P, PACK], F32, name="rec")
+        nc.vector.reciprocal(rec[:], den[:])
+        sj = sb.tile([P, PACK], F32, name="sj")
+        nc.vector.tensor_tensor(sj[:], rec[:], cj[:], ALU.mult)
+
+        def centre(h):
+            gsum = sb.tile([P, J // SET], F32, name=f"gsum{h}")
+            nc.vector.tensor_reduce(gsum[:], gg[h][:].rearrange("p (c e) -> p c e", e=SET), AX.X, ALU.add)
+            neg = sb.tile([P, J // SET, 2], F32, name=f"neg{h}")
+            nc.vector.tensor_scalar(neg[:], gsum[:].unsqueeze(2).to_broadcast([P, J // SET, 2]), -1.0 / SET, None, ALU.mult)
+            bank = ps.tile([P, PACK, P], F32, name=f"gbank{h}", tag=f"g{h}")
+            for s in range(PACK):
+                nc.tensor.matmul(bank[:, s, :], gg[h][:, s::PACK], ident[:], is_transpose=True, start=(s == 0), stop=False)
+            for s in range(PACK):
+                nc.tensor.matmul(bank[:, s, :], neg[:].rearrange("p c e -> p (c e)"), ident[:], is_transpose=True,
+                                 start=False, stop=(s == PACK - 1))
+            return bank
+
+        def weigh(name, bank, factor):
+            grouped = sb.tile([P, P, PACK], BF16, name=name, align_bytes=64)
+            nc.vector.tensor_tensor(grouped[:], bank[:].rearrange("p s c -> p c s"),
+                                    factor[:].unsqueeze(1).to_broadcast([P, P, PACK]), ALU.mult)
+            return grouped
+
+        def quantise(name, grouped, fmt):
+            codes = sb.tile([P, P], U32, name=name + "c", align_bytes=64)
+            plane = sb.tile([P, P], U8, name=name + "s", align_bytes=64)
+            nc.vector.quantize_mx(out=codes[:].bitcast(fmt), scales=plane[:], in_=grouped[:].rearrange("p c s -> p (c s)"))
+            return codes, plane
+
+        gbank0 = centre(0)
+        ub = [weigh("ub0", ubank[0], sj)]
+        uq = []
+        for t in range(1, PACK):
+            ub.append(weigh(f"ub{t}", ubank[t], sj))
+            uq.append(quantise(f"uq{t - 1}", ub[t - 1], E4M3))
+            if t == 1:
+                gbank1 = centre(1)
+        gb0 = weigh("gb0", gbank0, rj)
+        uq.append(quantise("uq3", ub[3], E4M3))
+        gq0 = quantise("gq0", gb0, E5M2)
+        gb1 = weigh("gb1", gbank1, rj)
+        gq1 = quantise("gq1", gb1, E5M2)
+        gq = [gq0, gq1]
+
+        half_old = sb.tile([P, 2, N], F32, name="half_old")
+        nc.scalar.activation(half_old[:], oldt[:], ACT.Copy, scale=0.5)
+
+        out_rows = out.rearrange("(a p) n -> p a n", p=P)
+        for h in range(2):
+            wbank = ps.tile([P, PACK, P], F32, name=f"wbank{h}", tag=("w" if h == 0 else "a"))
+            for t in range(PACK):
+                nc.tensor.matmul_mx(out=wbank[:, t, :], lhsT=uq[t][0][:].bitcast(E4M3), lhsT_scale=uq[t][1][:],
+                                    rhs=gq[h][0][:].bitcast(E5M2), rhs_scale=gq[h][1][:], start=True, stop=True)
+            wb = sb.tile([P, P, PACK], BF16, name=f"wb{h}", align_bytes=64)
+            nc.scalar.copy(wb[:], wbank[:].rearrange("p t c -> p c t"))
+            wc, wp = quantise(f"wq{h}", wb, E5M2)
+            vbank = ps.tile([P, 2, P], F32, name=f"vbank{h}", tag=f"g{h}")
+            for a in range(2):
+                nc.tensor.matmul_mx(out=vbank[:, a, :], lhsT=dwords[:, 2 * P * a:2 * P * (a + 1)].bitcast(E2M1),
+                                    lhsT_scale=dplane[:, P * a:P * (a + 1)],
+                                    rhs=wc[:].bitcast(E5M2), rhs_scale=wp[:], start=True, stop=True)
+            y = sb.tile([P, 2, P], F32, name=f"y{h}")
+            nc.vector.scalar_tensor_tensor(y[:], vbank[:], 0.05, half_old[:, :, P * h:P * (h + 1)], ALU.mult, ALU.add)
+            nc.sync.dma_start(out_rows[:, :, P * h:P * (h + 1)], y[:])

@@ -22,7 +22,8 @@ AX = mybir.AxisListType
 P = 128
 PACK = 4
 SET = 8
-VCOLS = 20
+VCOLS = (16, 32, 32, 32)
+GCOLS = None
 
 
 def tile_list_directions_sized_centred_mixed_kernel(tc, xf, ca, gt, rb, fkr, dr_words, dr_scales, old, offs, offs2, out):
@@ -31,28 +32,31 @@ def tile_list_directions_sized_centred_mixed_kernel(tc, xf, ca, gt, rb, fkr, dr_
         sb = ctx.enter_context(tc.tile_pool(name="sb", bufs=1))
         ps = ctx.enter_context(tc.psum_pool(name="ps", bufs=1))
 
+        def tile(name, shape, dtype, tag=None):
+            return sb.tile(shape, dtype, name=name, tag=tag or name, align_bytes=64)
+
         xlist = sb.tile([P, J // 16], U16, name="xlist")
         glist = sb.tile([P, J // 16], U16, name="glist")
-        xwin = [sb.tile([P, T], F32, name=f"xwin{t}") for t in range(PACK)]
-        gwin = [sb.tile([P, T], F32, name=f"gwin{h}") for h in range(2)]
-        fk = sb.tile([P, PACK], F32, name="fk")
-        cj = sb.tile([P, PACK], F32, name="cj")
-        rj = sb.tile([P, PACK], F32, name="rj")
-        oldt = sb.tile([P, 2, N], F32, name="oldt")
-        dwords = sb.tile([P, 2 * R], U8, name="dwords", align_bytes=64)
-        dplane = sb.tile([P, R], U8, name="dplane", align_bytes=64)
-        ident = sb.tile([P, P], F32, name="ident")
+        xwin = [tile(f"xwin{t}", [P, T], F32) for t in range(PACK)]
+        gwin = [tile(f"gwin{h}", [P, T], F32) for h in range(2)]
+        fk = tile("fk", [P, PACK], F32)
+        cj = tile("cj", [P, PACK], F32)
+        rj = tile("rj", [P, PACK], F32)
+        oldt = tile("oldt", [P, 2, N], F32)
+        dwords = tile("dwords", [P, 2 * R], U8)
+        dplane = tile("dplane", [P, R], U8)
+        ident = tile("ident", [P, P], F32)
 
         xrows = xf.rearrange("(p t) c -> t p c", t=PACK)
-        nc.sync.dma_start(xlist[:], offs)
         nc.sync.dma_start(xwin[0][:], xrows[0])
+        nc.sync.dma_start(xlist[:], offs)
         nc.scalar.dma_start(fk[:], fkr.rearrange("o (p t) -> p (o t)", t=PACK))
         for t in range(1, PACK):
             nc.sync.dma_start(xwin[t][:], xrows[t])
         nc.sync.dma_start(glist[:], offs2)
         nc.sync.dma_start(gwin[0][:], gt[0:P, :])
-        nc.sync.dma_start(cj[:], ca.rearrange("(p s) o -> p (s o)", s=PACK))
         nc.sync.dma_start(gwin[1][:], gt[P:2 * P, :])
+        nc.sync.dma_start(cj[:], ca.rearrange("(p s) o -> p (s o)", s=PACK))
         nc.sync.dma_start(rj[:], rb.rearrange("o (p s) -> p (o s)", s=PACK))
         nc.sync.dma_start(oldt[:], old.rearrange("(a p) n -> p a n", p=P))
         nc.sync.dma_start(dwords[:].bitcast(I32), dr_words[0].bitcast(I32))
@@ -63,43 +67,29 @@ def tile_list_directions_sized_centred_mixed_kernel(tc, xf, ca, gt, rb, fkr, dr_
 
         ubank = [ps.tile([P, PACK, P], F32, name=f"ubank{t}", tag=f"u{t}") for t in range(PACK)]
         abank = ps.tile([P, PACK, P], F32, name="abank", tag="a")
-        nv = 16 * VCOLS
-        for t in range(PACK):
-            xg = sb.tile([P, J], F32, name=f"xg{t}")
-            nc.vector.tensor_copy(xg[:, :nv], xwin[t][:].indirect(xlist[:, :VCOLS]))
-            nc.scalar.activation(xg[:, nv:], xwin[t][:].indirect(xlist[:, VCOLS:]), ACT.Copy)
-            by_slot = xg[:].rearrange("p (q s) -> p q s", s=PACK)
-            xa = sb.tile([P, PACK, P], F32, name=f"xa{t}")
-            nc.scalar.activation(xa[:].rearrange("p s q -> p q s"), by_slot, ACT.Abs, scale=1.0 / K)
-            xs = sb.tile([P, PACK, P], F32, name=f"xs{t}")
-            nc.vector.tensor_scalar(xs[:].rearrange("p s q -> p q s"), by_slot, fk[:, t:t + 1], None, ALU.mult)
-            for s in range(PACK):
-                nc.tensor.matmul(abank[:, s, :], xa[:, s, :], ident[:], is_transpose=True,
-                                 start=(t == 0 and s == 0), stop=(t == PACK - 1 and s == PACK - 1))
-            for s in range(PACK):
-                nc.tensor.transpose(ubank[t][:, s, :], xs[:, s, :], ident[:])
+        ones = tile("ones", [P, P], F32)
+        nc.vector.memset(ones[:], 1.0)
+        tenth = tile("tenth", [P, P], F32)
+        nc.scalar.activation(tenth[:], ones[:], ACT.Copy, scale=0.1 / P)
+        for s in range(PACK):
+            nc.tensor.matmul(abank[:, s, :], tenth[:], ident[:], is_transpose=True, start=(s == 0), stop=False)
 
-        gg = []
-        for h in range(2):
-            g = sb.tile([P, J], F32, name=f"gg{h}")
-            nc.scalar.activation(g[:], gwin[h][:].indirect(glist[:]), ACT.Copy)
-            gg.append(g)
+        def gather(name, window, entries, cols):
+            dense = tile(name, [P, J], F32)
+            nc.vector.tensor_copy(dense[:, :16 * cols], window[:].indirect(entries[:, :cols]))
+            if cols < J // 16:
+                nc.scalar.activation(dense[:, 16 * cols:], window[:].indirect(entries[:, cols:]), ACT.Copy)
+            return dense
 
-        mean = sb.tile([P, PACK], F32, name="mean")
-        nc.vector.tensor_reduce(mean[:], abank[:], AX.X, ALU.add)
-        den = sb.tile([P, PACK], F32, name="den")
-        nc.vector.tensor_scalar(den[:], mean[:], 0.1, None, ALU.add)
-        rec = sb.tile([P, PACK], F32, name="rec")
-        nc.vector.reciprocal(rec[:], den[:])
-        sj = sb.tile([P, PACK], F32, name="sj")
-        nc.vector.tensor_tensor(sj[:], rec[:], cj[:], ALU.mult)
-
-        def centre(h):
-            gsum = sb.tile([P, J // SET], F32, name=f"gsum{h}")
+        def sum_sets(h, tag):
+            gsum = tile(f"gsum{h}", [P, J // SET], F32, tag)
             nc.vector.tensor_reduce(gsum[:], gg[h][:].rearrange("p (c e) -> p c e", e=SET), AX.X, ALU.add)
-            neg = sb.tile([P, J // SET, 2], F32, name=f"neg{h}")
+            return gsum
+
+        def centre(h, gsum, bank_tag):
+            neg = tile(f"neg{h}", [P, J // SET, 2], F32)
             nc.vector.tensor_scalar(neg[:], gsum[:].unsqueeze(2).to_broadcast([P, J // SET, 2]), -1.0 / SET, None, ALU.mult)
-            bank = ps.tile([P, PACK, P], F32, name=f"gbank{h}", tag=f"g{h}")
+            bank = ps.tile([P, PACK, P], F32, name=f"gbank{h}", tag=bank_tag)
             for s in range(PACK):
                 nc.tensor.matmul(bank[:, s, :], gg[h][:, s::PACK], ident[:], is_transpose=True, start=(s == 0), stop=False)
             for s in range(PACK):
@@ -107,50 +97,106 @@ def tile_list_directions_sized_centred_mixed_kernel(tc, xf, ca, gt, rb, fkr, dr_
                                  start=False, stop=(s == PACK - 1))
             return bank
 
-        def weigh(name, bank, factor):
-            grouped = sb.tile([P, P, PACK], BF16, name=name, align_bytes=64)
-            nc.vector.tensor_tensor(grouped[:], bank[:].rearrange("p s c -> p c s"),
+        picked = []
+
+        def gather_x(t):
+            xg = gather(f"xg{t}", xwin[t], xlist, VCOLS[t])
+            by_slot = xg[:].rearrange("p (q s) -> p q s", s=PACK)
+            picked.append(by_slot)
+            xa = tile(f"xa{t}", [P, PACK, P], F32)
+            nc.scalar.activation(xa[:].rearrange("p s q -> p q s"), by_slot, ACT.Abs, scale=1.0 / K)
+            for s in range(PACK):
+                nc.tensor.matmul(abank[:, s, :], xa[:, s, :], ident[:], is_transpose=True,
+                                 start=False, stop=(t == PACK - 1 and s == PACK - 1))
+
+        def factor_x(t, xs):
+            if t < PACK - 1:
+                nc.scalar.activation(xs.rearrange("p s q -> p q s"), picked[t], ACT.Copy, scale=fk[:, t:t + 1])
+            else:
+                nc.vector.tensor_scalar(xs.rearrange("p s q -> p q s"), picked[t], fk[:, t:t + 1], None, ALU.mult)
+            for s in range(PACK):
+                nc.tensor.transpose(ubank[t][:, s, :], xs[:, s, :], ident[:])
+
+        def weigh_on_vector(grouped, bank, factor):
+            nc.vector.tensor_tensor(grouped, bank[:].rearrange("p s c -> p c s"),
                                     factor[:].unsqueeze(1).to_broadcast([P, P, PACK]), ALU.mult)
             return grouped
 
+        def weigh_on_scalar(grouped, flat, bank, factor):
+            for s in range(PACK):
+                nc.scalar.activation(flat[:, s, :], bank[:, s, :], ACT.Copy, scale=factor[:, s:s + 1])
+            nc.scalar.copy(grouped, flat.rearrange("p s c -> p c s"))
+            return grouped
+
         def quantise(name, grouped, fmt):
-            codes = sb.tile([P, P], U32, name=name + "c", align_bytes=64)
-            plane = sb.tile([P, P], U8, name=name + "s", align_bytes=64)
-            nc.vector.quantize_mx(out=codes[:].bitcast(fmt), scales=plane[:], in_=grouped[:].rearrange("p c s -> p (c s)"))
+            codes = tile(name + "c", [P, grouped.shape[1]], U32)
+            plane = tile(name + "s", [P, grouped.shape[1]], U8)
+            nc.vector.quantize_mx(out=codes[:].bitcast(fmt), scales=plane[:], in_=grouped.rearrange("p c s -> p (c s)"))
             return codes, plane
 
-        gbank0 = centre(0)
-        ub = [weigh("ub0", ubank[0], sj)]
-        uq = []
-        for t in range(1, PACK):
-            ub.append(weigh(f"ub{t}", ubank[t], sj))
-            uq.append(quantise(f"uq{t - 1}", ub[t - 1], E4M3))
-            if t == 1:
-                gbank1 = centre(1)
-        gb0 = weigh("gb0", gbank0, rj)
-        uq.append(quantise("uq3", ub[3], E4M3))
+        def words(name, tag=None):
+            return tile(name, [P, P, PACK], BF16, tag)[:]
+
+        def slots(name, dtype, tag=None):
+            return tile(name, [P, PACK, P], dtype, tag)[:]
+
+        for t in range(PACK):
+            gather_x(t)
+            factor_x(t, slots(f"xs{t}", F32))
+        gg = [tile("gg0", [P, J], F32, "fk"), tile("gg1", [P, J], F32, "xg3")]
+        nc.vector.tensor_copy(gg[0][:], gwin[0][:].indirect(glist[:]))
+        nc.scalar.activation(gg[1][:], gwin[1][:].indirect(glist[:]), ACT.Copy)
+
+        den = tile("den", [P, PACK], F32)
+        nc.vector.tensor_reduce(den[:], abank[:], AX.X, ALU.add)
+        gsum0 = sum_sets(0, "xa3")
+        rec = tile("rec", [P, PACK], F32)
+        nc.vector.reciprocal(rec[:], den[:])
+        gbank0 = centre(0, gsum0, "g0")
+        sj = tile("sj", [P, PACK], F32)
+        nc.vector.tensor_tensor(sj[:], rec[:], cj[:], ALU.mult)
+
+
+        half_old = tile("half_old", [P, 2, N], F32)
+        nc.gpsimd.tensor_scalar(half_old[:], oldt[:], 0.5, 0.0, ALU.mult, ALU.add)
+
+        pair = [tile(f"pair{i}", [P, 2 * P, PACK], BF16) for i in range(2)]
+        weigh_on_scalar(pair[1][:, :P, :], slots("ub0f", BF16, "gwin1"), ubank[0], sj)
+        gsum1 = sum_sets(1, "rec")
+        weigh_on_vector(pair[0][:, :P, :], ubank[1], sj)
+        gbank1 = centre(1, gsum1, "g1")
+        gb0 = weigh_on_scalar(words("gb0"), slots("gb0f", BF16, "gwin1"), gbank0, rj)
+        weigh_on_vector(pair[0][:, P:, :], ubank[2], sj)
+        weigh_on_vector(pair[1][:, P:, :], ubank[3], sj)
+        c12, s12 = quantise("uq12", pair[0][:], E4M3)
+        gb1 = weigh_on_vector(words("gb1"), gbank1, rj)
+        c03, s03 = quantise("uq03", pair[1][:], E4M3)
         gq0 = quantise("gq0", gb0, E5M2)
-        gb1 = weigh("gb1", gbank1, rj)
         gq1 = quantise("gq1", gb1, E5M2)
+        uq = [(c03[:, :P], s03[:, :P]), (c12[:, :P], s12[:, :P]), (c12[:, P:], s12[:, P:]), (c03[:, P:], s03[:, P:])]
         gq = [gq0, gq1]
 
-        half_old = sb.tile([P, 2, N], F32, name="half_old")
-        nc.scalar.activation(half_old[:], oldt[:], ACT.Copy, scale=0.5)
 
         out_rows = out.rearrange("(a p) n -> p a n", p=P)
+        wbank = [ps.tile([P, PACK, P], F32, name=f"wbank{h}", tag=("w", "a")[h]) for h in range(2)]
         for h in range(2):
-            wbank = ps.tile([P, PACK, P], F32, name=f"wbank{h}", tag=("w" if h == 0 else "a"))
-            for t in range(PACK):
-                nc.tensor.matmul_mx(out=wbank[:, t, :], lhsT=uq[t][0][:].bitcast(E4M3), lhsT_scale=uq[t][1][:],
+            for t in (1, 2, 0, 3):
+                nc.tensor.matmul_mx(out=wbank[h][:, t, :], lhsT=uq[t][0].bitcast(E4M3), lhsT_scale=uq[t][1],
                                     rhs=gq[h][0][:].bitcast(E5M2), rhs_scale=gq[h][1][:], start=True, stop=True)
-            wb = sb.tile([P, P, PACK], BF16, name=f"wb{h}", align_bytes=64)
-            nc.scalar.copy(wb[:], wbank[:].rearrange("p t c -> p c t"))
-            wc, wp = quantise(f"wq{h}", wb, E5M2)
+        wb = [words("wb0"), words("wb1")]
+        nc.scalar.copy(wb[0], wbank[0][:].rearrange("p t c -> p c t"))
+        nc.vector.tensor_copy(wb[1], wbank[1][:].rearrange("p t c -> p c t"))
+        vbanks = []
+        for h in range(2):
+            wc, wp = quantise(f"wq{h}", wb[h], E5M2)
             vbank = ps.tile([P, 2, P], F32, name=f"vbank{h}", tag=f"g{h}")
             for a in range(2):
                 nc.tensor.matmul_mx(out=vbank[:, a, :], lhsT=dwords[:, 2 * P * a:2 * P * (a + 1)].bitcast(E2M1),
                                     lhsT_scale=dplane[:, P * a:P * (a + 1)],
                                     rhs=wc[:].bitcast(E5M2), rhs_scale=wp[:], start=True, stop=True)
-            y = sb.tile([P, 2, P], F32, name=f"y{h}")
-            nc.vector.scalar_tensor_tensor(y[:], vbank[:], 0.05, half_old[:, :, P * h:P * (h + 1)], ALU.mult, ALU.add)
-            nc.sync.dma_start(out_rows[:, :, P * h:P * (h + 1)], y[:])
+            vbanks.append(vbank)
+        for h in range(2):
+            y = tile(f"y{h}", [P, 2, P], F32)
+            nc.vector.scalar_tensor_tensor(y[:], vbanks[h][:], 0.05, half_old[:, :, P * h:P * (h + 1)], ALU.mult, ALU.add)
+            queue = nc.sync if h == 0 else nc.scalar
+            queue.dma_start(out_rows[:, :, P * h:P * (h + 1)], y[:])

@@ -65,7 +65,8 @@ def tile_list_directions_sized_centred_mixed_kernel(tc, xf, ca, gt, rb, fkr, dr_
         for q in range(4):
             nc.sync.dma_start(dplane[32 * q:32 * q + 4, :].bitcast(I32), dr_scales[0, 4 * q:4 * q + 4, :].bitcast(I32))
 
-        ubank = [ps.tile([P, PACK, P], F32, name=f"ubank{t}", tag=f"u{t}") for t in range(PACK)]
+        early = [ps.tile([P, 2, 2, P], F32, name=f"early{i}", tag=f"u{i}") for i in range(2)]
+        late = [ps.tile([P, PACK, P], F32, name=f"late{i}", tag=f"u{2 + i}") for i in range(2)]
         abank = ps.tile([P, PACK, P], F32, name="abank", tag="a")
         ones = tile("ones", [P, P], F32)
         nc.vector.memset(ones[:], 1.0)
@@ -86,10 +87,10 @@ def tile_list_directions_sized_centred_mixed_kernel(tc, xf, ca, gt, rb, fkr, dr_
             nc.vector.tensor_reduce(gsum[:], gg[h][:].rearrange("p (c e) -> p c e", e=SET), AX.X, ALU.add)
             return gsum
 
-        def centre(h, gsum, bank_tag):
-            neg = tile(f"neg{h}", [P, J // SET, 2], F32)
+        def centre(h, gsum, tag):
+            neg = tile(f"neg{h}", [P, J // SET, 2], F32, tag)
             nc.vector.tensor_scalar(neg[:], gsum[:].unsqueeze(2).to_broadcast([P, J // SET, 2]), -1.0 / SET, None, ALU.mult)
-            bank = ps.tile([P, PACK, P], F32, name=f"gbank{h}", tag=bank_tag)
+            bank = ps.tile([P, PACK, P], F32, name=f"gbank{h}", tag=("a", "g")[h])
             for s in range(PACK):
                 nc.tensor.matmul(bank[:, s, :], gg[h][:, s::PACK], ident[:], is_transpose=True, start=(s == 0), stop=False)
             for s in range(PACK):
@@ -110,23 +111,16 @@ def tile_list_directions_sized_centred_mixed_kernel(tc, xf, ca, gt, rb, fkr, dr_
                                  start=False, stop=(t == PACK - 1 and s == PACK - 1))
 
         def factor_x(t, xs):
-            if t < PACK - 1:
-                nc.scalar.activation(xs.rearrange("p s q -> p q s"), picked[t], ACT.Copy, scale=fk[:, t:t + 1])
-            else:
-                nc.vector.tensor_scalar(xs.rearrange("p s q -> p q s"), picked[t], fk[:, t:t + 1], None, ALU.mult)
+            nc.scalar.activation(xs.rearrange("p s q -> p q s"), picked[t], ACT.Copy, scale=fk[:, t:t + 1])
             for s in range(PACK):
-                nc.tensor.transpose(ubank[t][:, s, :], xs[:, s, :], ident[:])
+                place = early[s // 2][:, s % 2, t, :] if t < 2 else late[t - 2][:, s, :]
+                nc.tensor.transpose(place, xs[:, s, :], ident[:])
 
         def weigh_on_vector(grouped, bank, factor):
             nc.vector.tensor_tensor(grouped, bank[:].rearrange("p s c -> p c s"),
                                     factor[:].unsqueeze(1).to_broadcast([P, P, PACK]), ALU.mult)
             return grouped
 
-        def weigh_on_scalar(grouped, flat, bank, factor):
-            for s in range(PACK):
-                nc.scalar.activation(flat[:, s, :], bank[:, s, :], ACT.Copy, scale=factor[:, s:s + 1])
-            nc.scalar.copy(grouped, flat.rearrange("p s c -> p c s"))
-            return grouped
 
         def quantise(name, grouped, fmt):
             codes = tile(name + "c", [P, grouped.shape[1]], U32)
@@ -142,54 +136,59 @@ def tile_list_directions_sized_centred_mixed_kernel(tc, xf, ca, gt, rb, fkr, dr_
 
         for t in range(PACK):
             gather_x(t)
+            if t < 2:
+                factor_x(t, slots(f"xs{t}", F32))
+        for t in range(2, PACK):
             factor_x(t, slots(f"xs{t}", F32))
-        gg = [tile("gg0", [P, J], F32, "fk"), tile("gg1", [P, J], F32, "xg3")]
+        gg = [tile("gg0", [P, J], F32), tile("gg1", [P, J], F32, "xg3")]
         nc.vector.tensor_copy(gg[0][:], gwin[0][:].indirect(glist[:]))
         nc.scalar.activation(gg[1][:], gwin[1][:].indirect(glist[:]), ACT.Copy)
 
+        gsum0 = sum_sets(0, None)
         den = tile("den", [P, PACK], F32)
         nc.vector.tensor_reduce(den[:], abank[:], AX.X, ALU.add)
-        gsum0 = sum_sets(0, "xa3")
+        gbank0 = centre(0, gsum0, "xa3")
         rec = tile("rec", [P, PACK], F32)
         nc.vector.reciprocal(rec[:], den[:])
-        gbank0 = centre(0, gsum0, "g0")
         sj = tile("sj", [P, PACK], F32)
         nc.vector.tensor_tensor(sj[:], rec[:], cj[:], ALU.mult)
 
 
-        half_old = tile("half_old", [P, 2, N], F32)
+        half_old = tile("half_old", [P, 2, N], F32, "cj")
         nc.gpsimd.tensor_scalar(half_old[:], oldt[:], 0.5, 0.0, ALU.mult, ALU.add)
 
         pair = [tile(f"pair{i}", [P, 2 * P, PACK], BF16) for i in range(2)]
-        weigh_on_scalar(pair[1][:, :P, :], slots("ub0f", BF16, "gwin1"), ubank[0], sj)
+        flat = tile("flat", [P, PACK, 2 * P], BF16, "gwin1")
+        for s in range(PACK):
+            nc.scalar.activation(flat[:, s, :], early[s // 2][:, s % 2, :, :].rearrange("p t c -> p (t c)"), ACT.Copy, scale=sj[:, s:s + 1])
+        nc.scalar.copy(pair[0][:], flat[:].rearrange("p s c -> p c s"))
+        weigh_on_vector(pair[1][:, :P, :], late[0], sj)
         gsum1 = sum_sets(1, "rec")
-        weigh_on_vector(pair[0][:, :P, :], ubank[1], sj)
-        gbank1 = centre(1, gsum1, "g1")
-        gb0 = weigh_on_scalar(words("gb0"), slots("gb0f", BF16, "gwin1"), gbank0, rj)
-        weigh_on_vector(pair[0][:, P:, :], ubank[2], sj)
-        weigh_on_vector(pair[1][:, P:, :], ubank[3], sj)
-        c12, s12 = quantise("uq12", pair[0][:], E4M3)
-        gb1 = weigh_on_vector(words("gb1"), gbank1, rj)
-        c03, s03 = quantise("uq03", pair[1][:], E4M3)
+        weigh_on_vector(pair[1][:, P:, :], late[1], sj)
+        gbank1 = centre(1, gsum1, None)
+        gb0 = weigh_on_vector(words("gb0"), gbank0, rj)
+        c23, s23 = quantise("uq23", pair[1][:], E4M3)
         gq0 = quantise("gq0", gb0, E5M2)
+        c01, s01 = quantise("uq01", pair[0][:], E4M3)
+        gb1 = weigh_on_vector(words("gb1"), gbank1, rj)
         gq1 = quantise("gq1", gb1, E5M2)
-        uq = [(c03[:, :P], s03[:, :P]), (c12[:, :P], s12[:, :P]), (c12[:, P:], s12[:, P:]), (c03[:, P:], s03[:, P:])]
+        uq = [(c01[:, :P], s01[:, :P]), (c01[:, P:], s01[:, P:]), (c23[:, :P], s23[:, :P]), (c23[:, P:], s23[:, P:])]
         gq = [gq0, gq1]
 
 
         out_rows = out.rearrange("(a p) n -> p a n", p=P)
-        wbank = [ps.tile([P, PACK, P], F32, name=f"wbank{h}", tag=("w", "a")[h]) for h in range(2)]
+        wbank = [ps.tile([P, PACK, P], F32, name=f"wbank{h}", tag=f"w{h}") for h in range(2)]
         for h in range(2):
-            for t in (1, 2, 0, 3):
+            for t in (2, 3, 0, 1):
                 nc.tensor.matmul_mx(out=wbank[h][:, t, :], lhsT=uq[t][0].bitcast(E4M3), lhsT_scale=uq[t][1],
                                     rhs=gq[h][0][:].bitcast(E5M2), rhs_scale=gq[h][1][:], start=True, stop=True)
         wb = [words("wb0"), words("wb1")]
         nc.scalar.copy(wb[0], wbank[0][:].rearrange("p t c -> p c t"))
-        nc.vector.tensor_copy(wb[1], wbank[1][:].rearrange("p t c -> p c t"))
+        nc.scalar.copy(wb[1], wbank[1][:].rearrange("p t c -> p c t"))
         vbanks = []
         for h in range(2):
             wc, wp = quantise(f"wq{h}", wb[h], E5M2)
-            vbank = ps.tile([P, 2, P], F32, name=f"vbank{h}", tag=f"g{h}")
+            vbank = ps.tile([P, 2, P], F32, name=f"vbank{h}", tag=f"u{h}")
             for a in range(2):
                 nc.tensor.matmul_mx(out=vbank[:, a, :], lhsT=dwords[:, 2 * P * a:2 * P * (a + 1)].bitcast(E2M1),
                                     lhsT_scale=dplane[:, P * a:P * (a + 1)],

from contextlib import ExitStack

import concourse.mybir as mybir
from concourse.masks import make_identity

K, J, N, R, T = 512, 512, 256, 256, 1024
FLOPS = 2 * J * K * N + 2 * K * R * N

F32 = mybir.dt.float32
BF16 = mybir.dt.bfloat16
I32 = mybir.dt.int32
U32 = mybir.dt.uint32
U16 = mybir.dt.uint16
U8 = mybir.dt.uint8
E4M3 = mybir.dt.float8_e4m3fn_x4
E5M2 = mybir.dt.float8_e5m2_x4
E2M1 = mybir.dt.float4_e2m1fn_x4
ALU = mybir.AluOpType
ACT = mybir.ActivationFunctionType
AX = mybir.AxisListType

P = 128
PACK = 4
SET = 8
VCOLS = (16, 32, 32, 32)
GCOLS = None


def tile_list_directions_sized_centred_mixed_kernel(tc, xf, ca, gt, rb, fkr, dr_words, dr_scales, old, offs, offs2, out):
    nc = tc.nc
    with ExitStack() as ctx:
        sb = ctx.enter_context(tc.tile_pool(name="sb", bufs=1))
        ps = ctx.enter_context(tc.psum_pool(name="ps", bufs=1))

        def tile(name, shape, dtype, tag=None):
            return sb.tile(shape, dtype, name=name, tag=tag or name, align_bytes=64)

        xlist = sb.tile([P, J // 16], U16, name="xlist")
        glist = sb.tile([P, J // 16], U16, name="glist")
        xwin = [tile(f"xwin{t}", [P, T], F32) for t in range(PACK)]
        gwin = [tile(f"gwin{h}", [P, T], F32) for h in range(2)]
        fk = tile("fk", [P, PACK], F32)
        cj = tile("cj", [P, PACK], F32)
        rj = tile("rj", [P, PACK], F32)
        oldt = tile("oldt", [P, 2, N], F32)
        dwords = tile("dwords", [P, 2 * R], U8)
        dplane = tile("dplane", [P, R], U8)
        ident = tile("ident", [P, P], F32)

        xrows = xf.rearrange("(p t) c -> t p c", t=PACK)
        nc.sync.dma_start(xwin[0][:], xrows[0])
        nc.sync.dma_start(xlist[:], offs)
        nc.scalar.dma_start(fk[:], fkr.rearrange("o (p t) -> p (o t)", t=PACK))
        for t in range(1, PACK):
            nc.sync.dma_start(xwin[t][:], xrows[t])
        nc.sync.dma_start(glist[:], offs2)
        nc.sync.dma_start(gwin[0][:], gt[0:P, :])
        nc.sync.dma_start(gwin[1][:], gt[P:2 * P, :])
        nc.sync.dma_start(cj[:], ca.rearrange("(p s) o -> p (s o)", s=PACK))
        nc.sync.dma_start(rj[:], rb.rearrange("o (p s) -> p (o s)", s=PACK))
        nc.sync.dma_start(oldt[:], old.rearrange("(a p) n -> p a n", p=P))
        nc.sync.dma_start(dwords[:].bitcast(I32), dr_words[0].bitcast(I32))
        make_identity(nc, ident[:])
        nc.gpsimd.memset(dplane[:].bitcast(I32), 0)
        for q in range(4):
            nc.sync.dma_start(dplane[32 * q:32 * q + 4, :].bitcast(I32), dr_scales[0, 4 * q:4 * q + 4, :].bitcast(I32))

        early = [ps.tile([P, 2, 2, P], F32, name=f"early{i}", tag=f"u{i}") for i in range(2)]
        late = [ps.tile([P, PACK, P], F32, name=f"late{i}", tag=f"u{2 + i}") for i in range(2)]
        abank = ps.tile([P, PACK, P], F32, name="abank", tag="a")
        ones = tile("ones", [P, P], F32)
        nc.vector.memset(ones[:], 1.0)
        tenth = tile("tenth", [P, P], F32)
        nc.scalar.activation(tenth[:], ones[:], ACT.Copy, scale=0.1 / P)
        for s in range(PACK):
            nc.tensor.matmul(abank[:, s, :], tenth[:], ident[:], is_transpose=True, start=(s == 0), stop=False)

        def gather(name, window, entries, cols):
            dense = tile(name, [P, J], F32)
            nc.vector.tensor_copy(dense[:, :16 * cols], window[:].indirect(entries[:, :cols]))
            if cols < J // 16:
                nc.scalar.activation(dense[:, 16 * cols:], window[:].indirect(entries[:, cols:]), ACT.Copy)
            return dense

        def sum_sets(h, tag):
            gsum = tile(f"gsum{h}", [P, J // SET], F32, tag)
            nc.vector.tensor_reduce(gsum[:], gg[h][:].rearrange("p (c e) -> p c e", e=SET), AX.X, ALU.add)
            return gsum

        def centre(h, gsum, tag):
            neg = tile(f"neg{h}", [P, J // SET, 2], F32, tag)
            nc.vector.tensor_scalar(neg[:], gsum[:].unsqueeze(2).to_broadcast([P, J // SET, 2]), -1.0 / SET, None, ALU.mult)
            bank = ps.tile([P, PACK, P], F32, name=f"gbank{h}", tag=("a", "g")[h])
            for s in range(PACK):
                nc.tensor.matmul(bank[:, s, :], gg[h][:, s::PACK], ident[:], is_transpose=True, start=(s == 0), stop=False)
            for s in range(PACK):
                nc.tensor.matmul(bank[:, s, :], neg[:].rearrange("p c e -> p (c e)"), ident[:], is_transpose=True,
                                 start=False, stop=(s == PACK - 1))
            return bank

        picked = []

        def gather_x(t):
            xg = gather(f"xg{t}", xwin[t], xlist, VCOLS[t])
            by_slot = xg[:].rearrange("p (q s) -> p q s", s=PACK)
            picked.append(by_slot)
            xa = tile(f"xa{t}", [P, PACK, P], F32)
            nc.scalar.activation(xa[:].rearrange("p s q -> p q s"), by_slot, ACT.Abs, scale=1.0 / K)
            for s in range(PACK):
                nc.tensor.matmul(abank[:, s, :], xa[:, s, :], ident[:], is_transpose=True,
                                 start=False, stop=(t == PACK - 1 and s == PACK - 1))

        def factor_x(t, xs):
            nc.scalar.activation(xs.rearrange("p s q -> p q s"), picked[t], ACT.Copy, scale=fk[:, t:t + 1])
            for s in range(PACK):
                place = early[s // 2][:, s % 2, t, :] if t < 2 else late[t - 2][:, s, :]
                nc.tensor.transpose(place, xs[:, s, :], ident[:])

        def weigh_on_vector(grouped, bank, factor):
            nc.vector.tensor_tensor(grouped, bank[:].rearrange("p s c -> p c s"),
                                    factor[:].unsqueeze(1).to_broadcast([P, P, PACK]), ALU.mult)
            return grouped


        def quantise(name, grouped, fmt):
            codes = tile(name + "c", [P, grouped.shape[1]], U32)
            plane = tile(name + "s", [P, grouped.shape[1]], U8)
            nc.vector.quantize_mx(out=codes[:].bitcast(fmt), scales=plane[:], in_=grouped.rearrange("p c s -> p (c s)"))
            return codes, plane

        def words(name, tag=None):
            return tile(name, [P, P, PACK], BF16, tag)[:]

        def slots(name, dtype, tag=None):
            return tile(name, [P, PACK, P], dtype, tag)[:]

        for t in range(PACK):
            gather_x(t)
            if t < 2:
                factor_x(t, slots(f"xs{t}", F32))
        for t in range(2, PACK):
            factor_x(t, slots(f"xs{t}", F32))
        gg = [tile("gg0", [P, J], F32), tile("gg1", [P, J], F32, "xg3")]
        nc.vector.tensor_copy(gg[0][:], gwin[0][:].indirect(glist[:]))
        nc.scalar.activation(gg[1][:], gwin[1][:].indirect(glist[:]), ACT.Copy)

        gsum0 = sum_sets(0, None)
        den = tile("den", [P, PACK], F32)
        nc.vector.tensor_reduce(den[:], abank[:], AX.X, ALU.add)
        gbank0 = centre(0, gsum0, "xa3")
        rec = tile("rec", [P, PACK], F32)
        nc.vector.reciprocal(rec[:], den[:])
        sj = tile("sj", [P, PACK], F32)
        nc.vector.tensor_tensor(sj[:], rec[:], cj[:], ALU.mult)


        half_old = tile("half_old", [P, 2, N], F32, "cj")
        nc.gpsimd.tensor_scalar(half_old[:], oldt[:], 0.5, 0.0, ALU.mult, ALU.add)

        pair = [tile(f"pair{i}", [P, 2 * P, PACK], BF16) for i in range(2)]
        flat = tile("flat", [P, PACK, 2 * P], BF16, "gwin1")
        for s in range(PACK):
            nc.scalar.activation(flat[:, s, :], early[s // 2][:, s % 2, :, :].rearrange("p t c -> p (t c)"), ACT.Copy, scale=sj[:, s:s + 1])
        nc.scalar.copy(pair[0][:], flat[:].rearrange("p s c -> p c s"))
        weigh_on_vector(pair[1][:, :P, :], late[0], sj)
        gsum1 = sum_sets(1, "rec")
        weigh_on_vector(pair[1][:, P:, :], late[1], sj)
        gbank1 = centre(1, gsum1, None)
        gb0 = weigh_on_vector(words("gb0"), gbank0, rj)
        c23, s23 = quantise("uq23", pair[1][:], E4M3)
        gq0 = quantise("gq0", gb0, E5M2)
        c01, s01 = quantise("uq01", pair[0][:], E4M3)
        gb1 = weigh_on_vector(words("gb1"), gbank1, rj)
        gq1 = quantise("gq1", gb1, E5M2)
        uq = [(c01[:, :P], s01[:, :P]), (c01[:, P:], s01[:, P:]), (c23[:, :P], s23[:, :P]), (c23[:, P:], s23[:, P:])]
        gq = [gq0, gq1]


        out_rows = out.rearrange("(a p) n -> p a n", p=P)
        wbank = [ps.tile([P, PACK, P], F32, name=f"wbank{h}", tag=f"w{h}") for h in range(2)]
        for h in range(2):
            for t in (2, 3, 0, 1):
                nc.tensor.matmul_mx(out=wbank[h][:, t, :], lhsT=uq[t][0].bitcast(E4M3), lhsT_scale=uq[t][1],
                                    rhs=gq[h][0][:].bitcast(E5M2), rhs_scale=gq[h][1][:], start=True, stop=True)
        wb = [words("wb0"), words("wb1")]
        nc.scalar.copy(wb[0], wbank[0][:].rearrange("p t c -> p c t"))
        nc.scalar.copy(wb[1], wbank[1][:].rearrange("p t c -> p c t"))
        vbanks = []
        for h in range(2):
            wc, wp = quantise(f"wq{h}", wb[h], E5M2)
            vbank = ps.tile([P, 2, P], F32, name=f"vbank{h}", tag=f"u{h}")
            for a in range(2):
                nc.tensor.matmul_mx(out=vbank[:, a, :], lhsT=dwords[:, 2 * P * a:2 * P * (a + 1)].bitcast(E2M1),
                                    lhsT_scale=dplane[:, P * a:P * (a + 1)],
                                    rhs=wc[:].bitcast(E5M2), rhs_scale=wp[:], start=True, stop=True)
            vbanks.append(vbank)
        for h in range(2):
            y = tile(f"y{h}", [P, 2, P], F32)
            nc.vector.scalar_tensor_tensor(y[:], vbanks[h][:], 0.05, half_old[:, :, P * h:P * (h + 1)], ALU.mult, ALU.add)
            queue = nc.sync if h == 0 else nc.scalar
            queue.dma_start(out_rows[:, :, P * h:P * (h + 1)], y[:])
